import numpy as np
import ml_dtypes


def mxq(x, axis, fmt="e4m3"):
    dtype, down = {"e4m3": (ml_dtypes.float8_e4m3fn, 7), "e5m2": (ml_dtypes.float8_e5m2, 14)}[fmt]
    v = np.moveaxis(np.asarray(x, np.float32).astype(ml_dtypes.bfloat16).astype(np.float64), axis, -1)
    blocks = v.reshape(v.shape[:-1] + (-1, 32))
    amax = np.abs(blocks).max(-1, keepdims=True)
    byte = np.maximum(np.where(amax > 0, np.frexp(amax)[1] - 1 + 127, 0) - down, 1)
    scale = np.exp2(byte - 127.0)
    codes = (blocks / scale).astype(np.float32).astype(dtype).astype(np.float64)
    return np.moveaxis((codes * scale).reshape(v.shape), -1, axis)


WIDE = False


def mx_kscale(k):
    if not WIDE:
        return np.ones(k)
    levels = np.array([10, -10, 5, -5, 0])
    if k % 512:
        return np.exp2(np.random.permutation(np.resize(levels, k // 32))).repeat(32)
    a = np.empty((k // 512, 16))
    for p in range(k // 512):
        a[p, :8] = np.random.permutation(np.resize(levels, 8))
        for g in range(8):
            far = levels[np.abs(levels - a[p, g]) >= 10]
            a[p, g + 8] = far[np.random.randint(len(far))]
    return np.exp2(a.ravel()).repeat(32)


def f64(x):
    return np.asarray(x).astype(np.float64)


def striped(idx):
    return np.tile(idx.reshape(-1, 16).T, (8, 1)).astype(np.uint16)


def unstriped(offs):
    return offs[:16].T.reshape(-1).astype(np.int64)


E2M1 = np.array([0.0, 0.5, 1.0, 1.5, 2.0, 3.0, 4.0, 6.0, -0.0, -0.5, -1.0, -1.5, -2.0, -3.0, -4.0, -6.0])


def pack_fp4(w):
    k, n = w.shape
    w = f64(np.asarray(w, np.float32).astype(ml_dtypes.bfloat16)).reshape(k // 32, 32, n)
    amax = np.abs(w).max(1)
    mant, ex = np.frexp(amax / 6.0)
    byte = np.clip(np.where(amax > 0, np.where(mant > 0.5, ex, ex - 1) + 127, 1), 1, 254)
    scaled = (w * np.exp2(127.0 - byte)[:, None, :]).reshape(k, n).astype(np.float32)
    c = np.ascontiguousarray(scaled.reshape(k // 512, 128, 4, n).transpose(0, 1, 3, 2)).astype(ml_dtypes.float4_e2m1fn).view(np.uint8) & 0xF
    words = (c[..., 0::2] | (c[..., 1::2] << 4)).reshape(k // 512, 128, 2 * n)
    return np.ascontiguousarray(words), np.ascontiguousarray(byte.astype(np.uint8).reshape(k // 512, 16, n))


def unpack_fp4(words, scales):
    g, _, n = scales.shape
    words = np.ascontiguousarray(words).reshape(g, 128, n, 2)
    nib = np.empty((g, 128, n, 4), np.uint8)
    nib[..., 0::2] = words & 0xF
    nib[..., 1::2] = words >> 4
    vals = E2M1[nib] * np.repeat(np.exp2(scales.astype(np.float64) - 127.0), 8, axis=1)[..., None]
    return vals.transpose(0, 1, 3, 2).reshape(g * 512, n)


K, T, N, U = 1024, 1024, 128, 2048
P = 2 ** 7


def setup_inputs():
    n = np.random.standard_normal
    s = mx_kscale(K)[:, None]
    packed_xT = pack_fp4(n((K, T)) * s)
    return {
        "x_words": packed_xT[0],
        "x_scales": packed_xT[1],
        "mem": n((N, U)).astype(np.float32),
        "w1": (n((K, N)) / np.sqrt(K) / s).astype(np.float32),
        "old": np.tile(np.random.uniform(0.5, 0.95, T), (P, 1)).astype(np.float32),
        "new": np.tile(np.random.uniform(0.05, 0.5, T), (P, 1)).astype(np.float32),
        "slot": striped(np.random.permutation(U)[:T]),
    }


def reference(x_words, x_scales, mem, w1, old, new, slot):
    xq = unpack_fp4(x_words, x_scales)
    y = np.tanh(mxq(f64(w1), 0, "e4m3").T @ xq)
    out = f64(mem).copy()
    out[:, unstriped(slot)] = f64(mem)[:, unstriped(slot)] * f64(old)[:1] + y * f64(new)[:1]
    return out

@@ -1,0 +1,136 @@
+from contextlib import ExitStack
+
+import concourse.mybir as mybir
+from concourse.masks import make_identity
+
+F32 = mybir.dt.float32
+BF16 = mybir.dt.bfloat16
+I32 = mybir.dt.int32
+U32 = mybir.dt.uint32
+U16 = mybir.dt.uint16
+U8 = mybir.dt.uint8
+FP8X4 = mybir.dt.float8_e4m3fn_x4
+FP4X4 = mybir.dt.float4_e2m1fn_x4
+MULT = mybir.AluOpType.mult
+ADD = mybir.AluOpType.add
+TANH = mybir.ActivationFunctionType.Tanh
+COPY = mybir.ActivationFunctionType.Copy
+
+P = 128
+K, T, M, U = 1024, 1024, 128, 2048
+PASSES = 2
+FLOPS = 2 * K * T * M
+BYTES = 2 * 128 * 2048 + 2 * 16 * 1024 + 2 * M * U * 4 + K * M * 4 + 2 * T * 4 + 128 * 64 * 2
+PIECES = ((0, 256, 128), (256, 512, 128), (512, 1024, 512))
+
+
+def tile_picked_wema_tanh_l_kernel(tc, x_words, x_scales, mem, w1, old, new, slot, out):
+    nc = tc.nc
+    with ExitStack() as ctx:
+        keep = ctx.enter_context(tc.tile_pool(name="keep", bufs=1))
+        psum = ctx.enter_context(tc.psum_pool(name="psum", bufs=1))
+
+        offsets = keep.tile([P, T // 16], U16, name="offsets")
+        window = keep.tile([P, U], F32, name="window")
+        old_cols = keep.tile([P, 2, 4], F32, name="old_cols")
+        new_cols = keep.tile([P, 2, 4], F32, name="new_cols", tag="new_cols", align_bytes=64)
+        ident = keep.tile([P, P], F32, name="ident")
+        x_plane = keep.tile([P, PASSES, T], U8, name="x_plane", align_bytes=64)
+
+        make_identity(nc, ident[:])
+
+        nc.scalar.dma_start(out=old_cols[:], in_=old[0].rearrange("(h p c) -> p h c", h=2, c=4))
+        nc.gpsimd.dma_start(out=new_cols[:], in_=new[0].rearrange("(h p c) -> p h c", h=2, c=4))
+        nc.sync.dma_start(offsets[:], slot)
+        nc.sync.dma_start(out=window[:], in_=mem)
+        w_raw = []
+        for z in range(PASSES):
+            raw = keep.tile([P, 4, M], F32, name="w_raw%d" % z)
+            nc.sync.dma_start(out=raw[:], in_=w1[512 * z : 512 * (z + 1), :].rearrange("(p j) m -> p j m", j=4))
+            w_raw.append(raw)
+        scale_rows = x_scales.bitcast(I32)
+        for q in range(4):
+            nc.sync.dma_start(
+                out=x_plane[32 * q : 32 * q + 4, :, :].bitcast(I32),
+                in_=scale_rows[:, 4 * q : 4 * q + 4, :].rearrange("z r c -> r z c"),
+            )
+        words = x_words.bitcast(I32).rearrange("z p c -> p z c")
+        x_codes = []
+        for i, (a, b) in enumerate(((0, 256), (256, T))):
+            codes = keep.tile([P, PASSES, 2 * (b - a)], U8, name="x_codes%d" % i, align_bytes=64)
+            nc.sync.dma_start(out=codes[:].bitcast(I32), in_=words[:, :, a // 2 : b // 2])
+            x_codes.append(codes)
+
+        old_rows = [keep.tile([P, 512], F32, name="old_rows%d" % h, tag="old_rows%d" % h, align_bytes=64) for h in range(2)]
+        new_banks = []
+        for h in range(2):
+            bank = psum.tile([P, 4, P], F32, name="old_bank%d" % h)
+            for c in range(4):
+                nc.tensor.transpose(bank[:, c, :], old_cols[:, h, c : c + 1].to_broadcast([P, P]), ident[:])
+            nc.vector.tensor_copy(out=old_rows[h][:].rearrange("q (p c) -> q p c", c=4), in_=bank[:].rearrange("q c p -> q p c"))
+        for h in range(2):
+            bank = psum.tile([P, 4, P], F32, name="new_bank%d" % h)
+            for c in range(4):
+                nc.tensor.transpose(bank[:, c, :], new_cols[:, h, c : c + 1].to_broadcast([P, P]), ident[:])
+            new_banks.append(bank)
+
+        def gather(dst, a, b):
+            h = a // 512
+            nc.vector.tensor_tensor(dst, window[:].indirect(offsets[:, a // 16 : b // 16]), old_rows[h][:, a - 512 * h : b - 512 * h], MULT)
+
+        kept = keep.tile([P, 768], F32, name="kept")
+        gather(kept[:, 0:512], 0, 512)
+        gather(kept[:, 512:768], 512, 768)
+
+        w_codes = keep.tile([P, PASSES, M], U32, name="w_codes", tag="old_rows0", align_bytes=64)
+        w_plane = keep.tile([P, PASSES, M], U8, name="w_plane", tag="new_cols", align_bytes=64)
+        for z in range(PASSES):
+            grouped = keep.tile([P, M, 4], BF16, name="w_grouped%d" % z, tag="w_grouped%d" % z, align_bytes=64)
+            nc.scalar.copy(
+                out=grouped[:].rearrange("p (c i) j -> p c j i", i=4),
+                in_=w_raw[z][:].rearrange("p j (c i) -> p c j i", i=4),
+            )
+            nc.vector.quantize_mx(
+                out=w_codes[:, z, :].bitcast(FP8X4), scales=w_plane[:, z, :], in_=grouped[:].rearrange("p m j -> p (m j)")
+            )
+
+        kept_last = keep.tile([P, 256], F32, name="kept_last", tag="w_grouped1", align_bytes=64)
+        gather(kept_last[:], 768, T)
+
+        y = keep.tile([P, T], F32, name="y")
+        moved = keep.tile([P, T], F32, name="moved")
+        for i, (a, b, n) in enumerate(PIECES):
+            acc = psum.tile([P, b - a], F32, name="acc%d" % i)
+            for g in range(0, b - a, n):
+                for z in range(PASSES):
+                    nc.tensor.matmul_mx(
+                        out=acc[:, g : g + n],
+                        lhsT=w_codes[:, z, :].bitcast(FP8X4),
+                        lhsT_scale=w_plane[:, z, :],
+                        rhs=x_codes[min(i, 1)][:, z, 2 * (g + a - 256 * min(i, 1)) : 2 * (g + n + a - 256 * min(i, 1))].bitcast(FP4X4),
+                        rhs_scale=x_plane[:, z, a + g : a + g + n],
+                        start=(z == 0),
+                        stop=(z == PASSES - 1),
+                    )
+            nc.scalar.activation(out=y[:, a:b], in_=acc[:], func=TANH)
+
+        def weigh(a, b):
+            h, lo, hi = a // 512, (a % 512) // 4, (a % 512) // 4 + (b - a) // 4
+            nc.vector.tensor_tensor(
+                moved[:, a:b].rearrange("q (p c) -> q p c", c=4),
+                new_banks[h][:].rearrange("q c p -> q p c")[:, lo:hi, :],
+                y[:, a:b].rearrange("q (p c) -> q p c", c=4),
+                MULT,
+            )
+
+        def scatter(src, a, b):
+            nc.vector.tensor_tensor(window[:].indirect(offsets[:, a // 16 : b // 16]), src, moved[:, a:b], ADD)
+
+        weigh(0, 256)
+        weigh(256, 512)
+        scatter(kept[:, 0:256], 0, 256)
+        weigh(512, T)
+        scatter(kept[:, 256:768], 256, 768)
+        scatter(kept_last[:], 768, T)
+
+        nc.sync.dma_start(out=out, in_=window[:])

@@ -14,7 +14,6 @@ FP4X4 = mybir.dt.float4_e2m1fn_x4
 MULT = mybir.AluOpType.mult
 ADD = mybir.AluOpType.add
 TANH = mybir.ActivationFunctionType.Tanh
-COPY = mybir.ActivationFunctionType.Copy
 
 P = 128
 K, T, M, U = 1024, 1024, 128, 2048
@@ -22,6 +21,7 @@ PASSES = 2
 FLOPS = 2 * K * T * M
 BYTES = 2 * 128 * 2048 + 2 * 16 * 1024 + 2 * M * U * 4 + K * M * 4 + 2 * T * 4 + 128 * 64 * 2
 PIECES = ((0, 256, 128), (256, 512, 128), (512, 1024, 512))
+FIRST = 256
 
 
 def tile_picked_wema_tanh_l_kernel(tc, x_words, x_scales, mem, w1, old, new, slot, out):
@@ -32,22 +32,19 @@ def tile_picked_wema_tanh_l_kernel(tc, x_words, x_scales, mem, w1, old, new, slo
 
         offsets = keep.tile([P, T // 16], U16, name="offsets")
         window = keep.tile([P, U], F32, name="window")
-        old_cols = keep.tile([P, 2, 4], F32, name="old_cols")
-        new_cols = keep.tile([P, 2, 4], F32, name="new_cols", tag="new_cols", align_bytes=64)
+        old_cols = keep.tile([P, 8], F32, name="old_cols")
+        new_cols = keep.tile([P, 8], F32, name="new_cols")
         ident = keep.tile([P, P], F32, name="ident")
         x_plane = keep.tile([P, PASSES, T], U8, name="x_plane", align_bytes=64)
+        w_raw = keep.tile([P, PASSES, 4, M], F32, name="w_raw")
 
         make_identity(nc, ident[:])
 
-        nc.scalar.dma_start(out=old_cols[:], in_=old[0].rearrange("(h p c) -> p h c", h=2, c=4))
-        nc.gpsimd.dma_start(out=new_cols[:], in_=new[0].rearrange("(h p c) -> p h c", h=2, c=4))
+        nc.sync.dma_start(out=old_cols[:], in_=old[0].rearrange("(p c) -> p c", c=8))
+        nc.sync.dma_start(out=w_raw[:], in_=w1.rearrange("(z p j) m -> p z j m", z=PASSES, j=4))
+        nc.sync.dma_start(out=new_cols[:], in_=new[0].rearrange("(p c) -> p c", c=8))
         nc.sync.dma_start(offsets[:], slot)
         nc.sync.dma_start(out=window[:], in_=mem)
-        w_raw = []
-        for z in range(PASSES):
-            raw = keep.tile([P, 4, M], F32, name="w_raw%d" % z)
-            nc.sync.dma_start(out=raw[:], in_=w1[512 * z : 512 * (z + 1), :].rearrange("(p j) m -> p j m", j=4))
-            w_raw.append(raw)
         scale_rows = x_scales.bitcast(I32)
         for q in range(4):
             nc.sync.dma_start(
@@ -55,82 +52,87 @@ def tile_picked_wema_tanh_l_kernel(tc, x_words, x_scales, mem, w1, old, new, slo
                 in_=scale_rows[:, 4 * q : 4 * q + 4, :].rearrange("z r c -> r z c"),
             )
         words = x_words.bitcast(I32).rearrange("z p c -> p z c")
-        x_codes = []
-        for i, (a, b) in enumerate(((0, 256), (256, T))):
-            codes = keep.tile([P, PASSES, 2 * (b - a)], U8, name="x_codes%d" % i, align_bytes=64)
-            nc.sync.dma_start(out=codes[:].bitcast(I32), in_=words[:, :, a // 2 : b // 2])
-            x_codes.append(codes)
+        x_first = keep.tile([P, PASSES, 2 * FIRST], U8, name="x_first", align_bytes=64)
+        nc.sync.dma_start(out=x_first[:].bitcast(I32), in_=words[:, :, : FIRST // 2])
+        x_rest = keep.tile([P, PASSES, 2 * (T - FIRST)], U8, name="x_rest", align_bytes=64)
+        nc.sync.dma_start(out=x_rest[:].bitcast(I32), in_=words[:, :, FIRST // 2 :])
 
-        old_rows = [keep.tile([P, 512], F32, name="old_rows%d" % h, tag="old_rows%d" % h, align_bytes=64) for h in range(2)]
-        new_banks = []
-        for h in range(2):
-            bank = psum.tile([P, 4, P], F32, name="old_bank%d" % h)
-            for c in range(4):
-                nc.tensor.transpose(bank[:, c, :], old_cols[:, h, c : c + 1].to_broadcast([P, P]), ident[:])
-            nc.vector.tensor_copy(out=old_rows[h][:].rearrange("q (p c) -> q p c", c=4), in_=bank[:].rearrange("q c p -> q p c"))
-        for h in range(2):
-            bank = psum.tile([P, 4, P], F32, name="new_bank%d" % h)
-            for c in range(4):
-                nc.tensor.transpose(bank[:, c, :], new_cols[:, h, c : c + 1].to_broadcast([P, P]), ident[:])
-            new_banks.append(bank)
+        def spread(cols, rows, name):
+            for h in range(2):
+                bank = psum.tile([P, 4, P], F32, name="%s_bank%d" % (name, h), tag="%s_bank%d" % (name, h))
+                for c in range(4):
+                    nc.tensor.transpose(bank[:, c, :], cols[:, 4 * h + c : 4 * h + c + 1].to_broadcast([P, P]), ident[:])
+                nc.scalar.copy(
+                    out=rows[:].rearrange("q (p c) -> q p c", c=8)[:, :, 4 * h : 4 * h + 4], in_=bank[:].rearrange("q c p -> q p c")
+                )
 
-        def gather(dst, a, b):
-            h = a // 512
-            nc.vector.tensor_tensor(dst, window[:].indirect(offsets[:, a // 16 : b // 16]), old_rows[h][:, a - 512 * h : b - 512 * h], MULT)
+        old_rows = keep.tile([P, T], F32, name="old_rows", tag="y2")
+        new_rows = keep.tile([P, T], F32, name="new_rows")
+        spread(old_cols, old_rows, "old")
+        spread(new_cols, new_rows, "new")
 
-        kept = keep.tile([P, 768], F32, name="kept")
-        gather(kept[:, 0:512], 0, 512)
-        gather(kept[:, 512:768], 512, 768)
-
-        w_codes = keep.tile([P, PASSES, M], U32, name="w_codes", tag="old_rows0", align_bytes=64)
-        w_plane = keep.tile([P, PASSES, M], U8, name="w_plane", tag="new_cols", align_bytes=64)
+        w_codes = keep.tile([P, PASSES, M], U32, name="w_codes", align_bytes=64)
+        w_plane = keep.tile([P, PASSES, M], U8, name="w_plane", align_bytes=64)
+        grouped = keep.tile([P, PASSES, M, 4], BF16, name="w_grouped", align_bytes=64)
         for z in range(PASSES):
-            grouped = keep.tile([P, M, 4], BF16, name="w_grouped%d" % z, tag="w_grouped%d" % z, align_bytes=64)
-            nc.scalar.copy(
-                out=grouped[:].rearrange("p (c i) j -> p c j i", i=4),
-                in_=w_raw[z][:].rearrange("p j (c i) -> p c j i", i=4),
+            nc.vector.tensor_copy(
+                out=grouped[:, z].rearrange("p (c i) j -> p c j i", i=4),
+                in_=w_raw[:, z].rearrange("p j (c i) -> p c j i", i=4),
             )
-            nc.vector.quantize_mx(
-                out=w_codes[:, z, :].bitcast(FP8X4), scales=w_plane[:, z, :], in_=grouped[:].rearrange("p m j -> p (m j)")
-            )
+        nc.vector.quantize_mx(
+            out=w_codes[:].rearrange("p z m -> p (z m)").bitcast(FP8X4),
+            scales=w_plane[:].rearrange("p z m -> p (z m)"),
+            in_=grouped[:].rearrange("p z m j -> p (z m j)"),
+        )
 
-        kept_last = keep.tile([P, 256], F32, name="kept_last", tag="w_grouped1", align_bytes=64)
-        gather(kept_last[:], 768, T)
+        ys = []
 
-        y = keep.tile([P, T], F32, name="y")
-        moved = keep.tile([P, T], F32, name="moved")
-        for i, (a, b, n) in enumerate(PIECES):
-            acc = psum.tile([P, b - a], F32, name="acc%d" % i)
-            for g in range(0, b - a, n):
+        def project(i):
+            a, b, n = PIECES[i]
+            acc = psum.tile([P, b - a], F32, name="acc%d" % i, tag="new_bank%d" % (i % 2))
+            for g in range(a, b, n):
                 for z in range(PASSES):
+                    codes = x_first[:, z, 2 * g : 2 * (g + n)] if i == 0 else x_rest[:, z, 2 * (g - FIRST) : 2 * (g - FIRST + n)]
                     nc.tensor.matmul_mx(
-                        out=acc[:, g : g + n],
+                        out=acc[:, g - a : g - a + n],
                         lhsT=w_codes[:, z, :].bitcast(FP8X4),
                         lhsT_scale=w_plane[:, z, :],
-                        rhs=x_codes[min(i, 1)][:, z, 2 * (g + a - 256 * min(i, 1)) : 2 * (g + n + a - 256 * min(i, 1))].bitcast(FP4X4),
-                        rhs_scale=x_plane[:, z, a + g : a + g + n],
+                        rhs=codes.bitcast(FP4X4),
+                        rhs_scale=x_plane[:, z, g : g + n],
                         start=(z == 0),
                         stop=(z == PASSES - 1),
                     )
-            nc.scalar.activation(out=y[:, a:b], in_=acc[:], func=TANH)
+            y = keep.tile([P, b - a], F32, name="y%d" % i, tag="y%d" % i)
+            nc.scalar.activation(out=y[:], in_=acc[:], func=TANH)
+            ys.append(y)
 
-        def weigh(a, b):
-            h, lo, hi = a // 512, (a % 512) // 4, (a % 512) // 4 + (b - a) // 4
-            nc.vector.tensor_tensor(
-                moved[:, a:b].rearrange("q (p c) -> q p c", c=4),
-                new_banks[h][:].rearrange("q c p -> q p c")[:, lo:hi, :],
-                y[:, a:b].rearrange("q (p c) -> q p c", c=4),
-                MULT,
-            )
+        project(0)
+        project(1)
+
+        moved_first = keep.tile([P, FIRST], F32, name="moved_first")
+        moved_rest = keep.tile([P, T - FIRST], F32, name="moved_rest")
+
+        def moved(a, b):
+            return moved_first[:, a:b] if a < FIRST else moved_rest[:, a - FIRST : b - FIRST]
+
+        def gather(dst, a, b):
+            nc.vector.tensor_tensor(dst, window[:].indirect(offsets[:, a // 16 : b // 16]), old_rows[:, a:b], MULT)
+
+        def weigh(i):
+            a, b, n = PIECES[i]
+            nc.vector.tensor_tensor(moved(a, b), ys[i][:], new_rows[:, a:b], MULT)
 
         def scatter(src, a, b):
-            nc.vector.tensor_tensor(window[:].indirect(offsets[:, a // 16 : b // 16]), src, moved[:, a:b], ADD)
+            nc.vector.tensor_tensor(window[:].indirect(offsets[:, a // 16 : b // 16]), src, moved(a, b), ADD)
 
-        weigh(0, 256)
-        weigh(256, 512)
+        kept = keep.tile([P, T], F32, name="kept")
+        gather(kept[:, 0:768], 0, 768)
+        weigh(0)
+        gather(kept[:, 768:T], 768, T)
+        project(2)
+        weigh(1)
         scatter(kept[:, 0:256], 0, 256)
-        weigh(512, T)
-        scatter(kept[:, 256:768], 256, 768)
-        scatter(kept_last[:], 768, T)
+        weigh(2)
+        scatter(kept[:, 256:T], 256, T)
 
         nc.sync.dma_start(out=out, in_=window[:])

@@ -14,14 +14,17 @@ FP4X4 = mybir.dt.float4_e2m1fn_x4
 MULT = mybir.AluOpType.mult
 ADD = mybir.AluOpType.add
 TANH = mybir.ActivationFunctionType.Tanh
+COPY = mybir.ActivationFunctionType.Copy
 
 P = 128
 K, T, M, U = 1024, 1024, 128, 2048
 PASSES = 2
 FLOPS = 2 * K * T * M
 BYTES = 2 * 128 * 2048 + 2 * 16 * 1024 + 2 * M * U * 4 + K * M * 4 + 2 * T * 4 + 128 * 64 * 2
-PIECES = ((0, 256, 128), (256, 512, 128), (512, 1024, 512))
-FIRST = 256
+WEIGHED = 512
+LOADS = ((0, 128), (128, WEIGHED), (WEIGHED, T))
+PIECES = ((0, 128, "acc0"), (128, 256, "acc1"), (256, 384, "old_bank0"), (384, WEIGHED, "old_bank1"))
+TURNED = ((0, 256, "new_bank"), (256, 512, "acc0"))
 
 
 def tile_picked_wema_tanh_l_kernel(tc, x_words, x_scales, mem, w1, old, new, slot, out):
@@ -33,16 +36,17 @@ def tile_picked_wema_tanh_l_kernel(tc, x_words, x_scales, mem, w1, old, new, slo
         offsets = keep.tile([P, T // 16], U16, name="offsets")
         window = keep.tile([P, U], F32, name="window")
         old_cols = keep.tile([P, 8], F32, name="old_cols")
-        new_cols = keep.tile([P, 8], F32, name="new_cols")
+        new_cols = keep.tile([P, 4], F32, name="new_cols")
+        new_scale = keep.tile([P, (T - WEIGHED) // P], F32, name="new_scale")
         ident = keep.tile([P, P], F32, name="ident")
         x_plane = keep.tile([P, PASSES, T], U8, name="x_plane", align_bytes=64)
         w_raw = keep.tile([P, PASSES, 4, M], F32, name="w_raw")
 
         make_identity(nc, ident[:])
 
-        nc.sync.dma_start(out=old_cols[:], in_=old[0].rearrange("(p c) -> p c", c=8))
         nc.sync.dma_start(out=w_raw[:], in_=w1.rearrange("(z p j) m -> p z j m", z=PASSES, j=4))
-        nc.sync.dma_start(out=new_cols[:], in_=new[0].rearrange("(p c) -> p c", c=8))
+        nc.sync.dma_start(out=old_cols[:], in_=old[0].rearrange("(p c) -> p c", c=8))
+        nc.sync.dma_start(out=new_cols[:], in_=new[0, 0:WEIGHED].rearrange("(p c) -> p c", c=4))
         nc.sync.dma_start(offsets[:], slot)
         nc.sync.dma_start(out=window[:], in_=mem)
         scale_rows = x_scales.bitcast(I32)
@@ -52,87 +56,102 @@ def tile_picked_wema_tanh_l_kernel(tc, x_words, x_scales, mem, w1, old, new, slo
                 in_=scale_rows[:, 4 * q : 4 * q + 4, :].rearrange("z r c -> r z c"),
             )
         words = x_words.bitcast(I32).rearrange("z p c -> p z c")
-        x_first = keep.tile([P, PASSES, 2 * FIRST], U8, name="x_first", align_bytes=64)
-        nc.sync.dma_start(out=x_first[:].bitcast(I32), in_=words[:, :, : FIRST // 2])
-        x_rest = keep.tile([P, PASSES, 2 * (T - FIRST)], U8, name="x_rest", align_bytes=64)
-        nc.sync.dma_start(out=x_rest[:].bitcast(I32), in_=words[:, :, FIRST // 2 :])
+        x_codes = []
+        for i, (a, b) in enumerate(LOADS):
+            piece = keep.tile([P, PASSES, 2 * (b - a)], U8, name="x_codes%d" % i, align_bytes=64)
+            nc.sync.dma_start(out=piece[:].bitcast(I32), in_=words[:, :, a // 2 : b // 2])
+            x_codes.append(piece)
+        with nc.allow_non_contiguous_dma(reason="one weight for each partition and block"):
+            nc.sync.dma_start(out=new_scale[:], in_=new[1, WEIGHED:T].rearrange("(b p) -> p b", p=P))
 
-        def spread(cols, rows, name):
-            for h in range(2):
-                bank = psum.tile([P, 4, P], F32, name="%s_bank%d" % (name, h), tag="%s_bank%d" % (name, h))
-                for c in range(4):
-                    nc.tensor.transpose(bank[:, c, :], cols[:, 4 * h + c : 4 * h + c + 1].to_broadcast([P, P]), ident[:])
-                nc.scalar.copy(
-                    out=rows[:].rearrange("q (p c) -> q p c", c=8)[:, :, 4 * h : 4 * h + 4], in_=bank[:].rearrange("q c p -> q p c")
-                )
+        def codes_of(z, g):
+            i = [a <= g < b for a, b in LOADS].index(True)
+            first = LOADS[i][0]
+            return x_codes[i][:, z, 2 * (g - first) : 2 * (g - first + P)].bitcast(FP4X4)
 
-        old_rows = keep.tile([P, T], F32, name="old_rows", tag="y2")
-        new_rows = keep.tile([P, T], F32, name="new_rows")
-        spread(old_cols, old_rows, "old")
-        spread(new_cols, new_rows, "new")
+        old_rows = keep.tile([P, T], F32, name="old_rows")
+        for h in range(2):
+            bank = psum.tile([P, 4, P], F32, name="old_bank%d" % h, tag="old_bank%d" % h)
+            for c in range(4):
+                nc.tensor.transpose(bank[:, c, :], old_cols[:, 4 * h + c : 4 * h + c + 1].to_broadcast([P, P]), ident[:])
+            nc.scalar.copy(
+                out=old_rows[:].rearrange("q (p c) -> q p c", c=8)[:, :, 4 * h : 4 * h + 4], in_=bank[:].rearrange("q c p -> q p c")
+            )
+        new_rows = keep.tile([P, WEIGHED], F32, name="new_rows")
+        bank = psum.tile([P, 4, P], F32, name="new_bank", tag="new_bank")
+        for c in range(4):
+            nc.tensor.transpose(bank[:, c, :], new_cols[:, c : c + 1].to_broadcast([P, P]), ident[:])
+        nc.scalar.copy(out=new_rows[:].rearrange("q (p c) -> q p c", c=4), in_=bank[:].rearrange("q c p -> q p c"))
 
-        w_codes = keep.tile([P, PASSES, M], U32, name="w_codes", align_bytes=64)
-        w_plane = keep.tile([P, PASSES, M], U8, name="w_plane", align_bytes=64)
         grouped = keep.tile([P, PASSES, M, 4], BF16, name="w_grouped", align_bytes=64)
         for z in range(PASSES):
             nc.vector.tensor_copy(
                 out=grouped[:, z].rearrange("p (c i) j -> p c j i", i=4),
                 in_=w_raw[:, z].rearrange("p j (c i) -> p c j i", i=4),
             )
+        w_words = keep.tile([P, PASSES, M], U32, name="w_words", align_bytes=64)
+        w_plane = keep.tile([P, PASSES, M], U8, name="w_plane", align_bytes=64)
         nc.vector.quantize_mx(
-            out=w_codes[:].rearrange("p z m -> p (z m)").bitcast(FP8X4),
+            out=w_words[:].rearrange("p z m -> p (z m)").bitcast(FP8X4),
             scales=w_plane[:].rearrange("p z m -> p (z m)"),
             in_=grouped[:].rearrange("p z m j -> p (z m j)"),
         )
 
-        ys = []
+        kept = keep.tile([P, T], F32, name="kept")
+        nc.vector.tensor_tensor(kept[:], window[:].indirect(offsets[:]), old_rows[:], MULT)
 
-        def project(i):
-            a, b, n = PIECES[i]
-            acc = psum.tile([P, b - a], F32, name="acc%d" % i, tag="new_bank%d" % (i % 2))
-            for g in range(a, b, n):
+        y = keep.tile([P, WEIGHED], F32, name="y")
+        for i, (a, b, tag) in enumerate(PIECES):
+            acc = psum.tile([P, b - a], F32, name="acc%d" % i, tag=tag)
+            for g in range(a, b, P):
                 for z in range(PASSES):
-                    codes = x_first[:, z, 2 * g : 2 * (g + n)] if i == 0 else x_rest[:, z, 2 * (g - FIRST) : 2 * (g - FIRST + n)]
                     nc.tensor.matmul_mx(
-                        out=acc[:, g - a : g - a + n],
-                        lhsT=w_codes[:, z, :].bitcast(FP8X4),
+                        out=acc[:, g - a : g - a + P],
+                        lhsT=w_words[:, z, :].bitcast(FP8X4),
                         lhsT_scale=w_plane[:, z, :],
-                        rhs=codes.bitcast(FP4X4),
-                        rhs_scale=x_plane[:, z, g : g + n],
+                        rhs=codes_of(z, g),
+                        rhs_scale=x_plane[:, z, g : g + P],
                         start=(z == 0),
                         stop=(z == PASSES - 1),
                     )
-            y = keep.tile([P, b - a], F32, name="y%d" % i, tag="y%d" % i)
-            nc.scalar.activation(out=y[:], in_=acc[:], func=TANH)
-            ys.append(y)
+            nc.scalar.activation(out=y[:, a:b], in_=acc[:], func=TANH)
 
-        project(0)
-        project(1)
+        moved = keep.tile([P, T], F32, name="moved")
+        y_t = keep.tile([P, T - WEIGHED], F32, name="y_t")
+        moved_t = keep.tile([P, T - WEIGHED], F32, name="moved_t")
+        for h, (a, b, tag) in enumerate(TURNED):
+            acc_t = psum.tile([P, b - a], F32, name="acc_t%d" % h, tag=tag)
+            for g in range(a, b, P):
+                for z in range(PASSES):
+                    nc.tensor.matmul_mx(
+                        out=acc_t[:, g - a : g - a + P],
+                        lhsT=codes_of(z, WEIGHED + g),
+                        lhsT_scale=x_plane[:, z, WEIGHED + g : WEIGHED + g + P],
+                        rhs=w_words[:, z, :].bitcast(FP8X4),
+                        rhs_scale=w_plane[:, z, :],
+                        start=(z == 0),
+                        stop=(z == PASSES - 1),
+                    )
+            nc.scalar.activation(out=y_t[:, a:b], in_=acc_t[:], func=TANH)
+        for g in range(0, T - WEIGHED, P):
+            nc.scalar.activation(out=moved_t[:, g : g + P], in_=y_t[:, g : g + P], func=COPY, scale=new_scale[:, g // P : g // P + 1])
+        for h, (a, b, tag) in enumerate(TURNED):
+            back = psum.tile([P, b - a], F32, name="back%d" % h, tag="back%d" % h)
+            for g in range(a, b, P):
+                nc.tensor.transpose(back[:, g - a : g - a + P], moved_t[:, g : g + P], ident[:])
+            nc.scalar.copy(out=moved[:, WEIGHED + a : WEIGHED + b], in_=back[:])
 
-        moved_first = keep.tile([P, FIRST], F32, name="moved_first")
-        moved_rest = keep.tile([P, T - FIRST], F32, name="moved_rest")
+        def weigh(a, b):
+            nc.vector.tensor_tensor(moved[:, a:b], y[:, a:b], new_rows[:, a:b], MULT)
 
-        def moved(a, b):
-            return moved_first[:, a:b] if a < FIRST else moved_rest[:, a - FIRST : b - FIRST]
+        def scatter(a, b):
+            nc.vector.tensor_tensor(window[:].indirect(offsets[:, a // 16 : b // 16]), kept[:, a:b], moved[:, a:b], ADD)
 
-        def gather(dst, a, b):
-            nc.vector.tensor_tensor(dst, window[:].indirect(offsets[:, a // 16 : b // 16]), old_rows[:, a:b], MULT)
-
-        def weigh(i):
-            a, b, n = PIECES[i]
-            nc.vector.tensor_tensor(moved(a, b), ys[i][:], new_rows[:, a:b], MULT)
-
-        def scatter(src, a, b):
-            nc.vector.tensor_tensor(window[:].indirect(offsets[:, a // 16 : b // 16]), src, moved(a, b), ADD)
-
-        kept = keep.tile([P, T], F32, name="kept")
-        gather(kept[:, 0:768], 0, 768)
-        weigh(0)
-        gather(kept[:, 768:T], 768, T)
-        project(2)
-        weigh(1)
-        scatter(kept[:, 0:256], 0, 256)
-        weigh(2)
-        scatter(kept[:, 256:T], 256, T)
-
+        weigh(0, 128)
+        weigh(128, 256)
+        weigh(256, 384)
+        scatter(0, 128)
+        weigh(384, WEIGHED)
+        scatter(128, 384)
+        scatter(384, T)
         nc.sync.dma_start(out=out, in_=window[:])

@@ -23,8 +23,9 @@ FLOPS = 2 * K * T * M
 BYTES = 2 * 128 * 2048 + 2 * 16 * 1024 + 2 * M * U * 4 + K * M * 4 + 2 * T * 4 + 128 * 64 * 2
 WEIGHED = 512
 LOADS = ((0, 128), (128, WEIGHED), (WEIGHED, T))
-PIECES = ((0, 128, "acc0"), (128, 256, "acc1"), (256, 384, "old_bank0"), (384, WEIGHED, "old_bank1"))
-TURNED = ((0, 256, "new_bank"), (256, 512, "acc0"))
+PIECES = ((0, 128, "acc0"), (128, 256, "acc1"), (256, 384, "old_bank0"), (384, WEIGHED, "new_bank"))
+TURNED = ((0, 256, "acc0"), (256, 512, "acc1"))
+FETCH = 256
 
 
 def tile_picked_wema_tanh_l_kernel(tc, x_words, x_scales, mem, w1, old, new, slot, out):
@@ -35,7 +36,7 @@ def tile_picked_wema_tanh_l_kernel(tc, x_words, x_scales, mem, w1, old, new, slo
 
         offsets = keep.tile([P, T // 16], U16, name="offsets")
         window = keep.tile([P, U], F32, name="window")
-        old_cols = keep.tile([P, 8], F32, name="old_cols")
+        old_cols = keep.tile([P, 2, 4], F32, name="old_cols", tag="old_cols")
         new_cols = keep.tile([P, 4], F32, name="new_cols")
         new_scale = keep.tile([P, (T - WEIGHED) // P], F32, name="new_scale")
         ident = keep.tile([P, P], F32, name="ident")
@@ -45,7 +46,7 @@ def tile_picked_wema_tanh_l_kernel(tc, x_words, x_scales, mem, w1, old, new, slo
         make_identity(nc, ident[:])
 
         nc.sync.dma_start(out=w_raw[:], in_=w1.rearrange("(z p j) m -> p z j m", z=PASSES, j=4))
-        nc.sync.dma_start(out=old_cols[:], in_=old[0].rearrange("(p c) -> p c", c=8))
+        nc.sync.dma_start(out=old_cols[:], in_=old[0].rearrange("(h p c) -> p h c", h=2, c=4))
         nc.sync.dma_start(out=new_cols[:], in_=new[0, 0:WEIGHED].rearrange("(p c) -> p c", c=4))
         nc.sync.dma_start(offsets[:], slot)
         nc.sync.dma_start(out=window[:], in_=mem)
@@ -69,19 +70,17 @@ def tile_picked_wema_tanh_l_kernel(tc, x_words, x_scales, mem, w1, old, new, slo
             first = LOADS[i][0]
             return x_codes[i][:, z, 2 * (g - first) : 2 * (g - first + P)].bitcast(FP4X4)
 
-        old_rows = keep.tile([P, T], F32, name="old_rows")
-        for h in range(2):
-            bank = psum.tile([P, 4, P], F32, name="old_bank%d" % h, tag="old_bank%d" % h)
+        def spread(cols, name):
+            bank = psum.tile([P, 4, P], F32, name=name, tag=name)
             for c in range(4):
-                nc.tensor.transpose(bank[:, c, :], old_cols[:, 4 * h + c : 4 * h + c + 1].to_broadcast([P, P]), ident[:])
-            nc.scalar.copy(
-                out=old_rows[:].rearrange("q (p c) -> q p c", c=8)[:, :, 4 * h : 4 * h + 4], in_=bank[:].rearrange("q c p -> q p c")
-            )
+                nc.tensor.transpose(bank[:, c, :], cols[:, c : c + 1].to_broadcast([P, P]), ident[:])
+            return bank[:].rearrange("q c p -> q p c")
+
+        old_rows = keep.tile([P, WEIGHED], F32, name="old_rows")
         new_rows = keep.tile([P, WEIGHED], F32, name="new_rows")
-        bank = psum.tile([P, 4, P], F32, name="new_bank", tag="new_bank")
-        for c in range(4):
-            nc.tensor.transpose(bank[:, c, :], new_cols[:, c : c + 1].to_broadcast([P, P]), ident[:])
-        nc.scalar.copy(out=new_rows[:].rearrange("q (p c) -> q p c", c=4), in_=bank[:].rearrange("q c p -> q p c"))
+        nc.scalar.copy(out=old_rows[:].rearrange("q (p c) -> q p c", c=4), in_=spread(old_cols[:, 0, :], "old_bank0"))
+        nc.scalar.copy(out=new_rows[:].rearrange("q (p c) -> q p c", c=4), in_=spread(new_cols[:], "new_bank"))
+        old_second = spread(old_cols[:, 1, :], "old_bank1")
 
         grouped = keep.tile([P, PASSES, M, 4], BF16, name="w_grouped", align_bytes=64)
         for z in range(PASSES):
@@ -98,9 +97,24 @@ def tile_picked_wema_tanh_l_kernel(tc, x_words, x_scales, mem, w1, old, new, slo
         )
 
         kept = keep.tile([P, T], F32, name="kept")
-        nc.vector.tensor_tensor(kept[:], window[:].indirect(offsets[:]), old_rows[:], MULT)
+        fetched = keep.tile([P, T - WEIGHED], F32, name="fetched", tag="old_cols")
 
-        y = keep.tile([P, WEIGHED], F32, name="y")
+        def entries(a, b):
+            return window[:].indirect(offsets[:, a // 16 : b // 16])
+
+        for a in range(0, WEIGHED, FETCH):
+            nc.vector.tensor_tensor(kept[:, a : a + FETCH], entries(a, a + FETCH), old_rows[:, a : a + FETCH], MULT)
+        for a in range(0, T - WEIGHED, FETCH):
+            b = a + FETCH
+            nc.scalar.activation(out=fetched[:, a:b], in_=entries(WEIGHED + a, WEIGHED + b), func=COPY)
+            nc.vector.tensor_tensor(
+                kept[:, WEIGHED + a : WEIGHED + b].rearrange("q (p c) -> q p c", c=4),
+                fetched[:, a:b].rearrange("q (p c) -> q p c", c=4),
+                old_second[:, a // 4 : b // 4, :],
+                MULT,
+            )
+
+        y = old_rows
         for i, (a, b, tag) in enumerate(PIECES):
             acc = psum.tile([P, b - a], F32, name="acc%d" % i, tag=tag)
             for g in range(a, b, P):
@@ -145,7 +159,7 @@ def tile_picked_wema_tanh_l_kernel(tc, x_words, x_scales, mem, w1, old, new, slo
             nc.vector.tensor_tensor(moved[:, a:b], y[:, a:b], new_rows[:, a:b], MULT)
 
         def scatter(a, b):
-            nc.vector.tensor_tensor(window[:].indirect(offsets[:, a // 16 : b // 16]), kept[:, a:b], moved[:, a:b], ADD)
+            nc.vector.tensor_tensor(entries(a, b), kept[:, a:b], moved[:, a:b], ADD)
 
         weigh(0, 128)
         weigh(128, 256)

@@ -23,7 +23,7 @@ FLOPS = 2 * K * T * M
 BYTES = 2 * 128 * 2048 + 2 * 16 * 1024 + 2 * M * U * 4 + K * M * 4 + 2 * T * 4 + 128 * 64 * 2
 WEIGHED = 512
 LOADS = ((0, 128), (128, WEIGHED), (WEIGHED, T))
-PIECES = ((0, 128, "acc0"), (128, 256, "acc1"), (256, 384, "old_bank0"), (384, WEIGHED, "new_bank"))
+PIECES = ((0, 128, "acc0"), (128, 256, "acc1"), (256, 384, "old_bank0"), (384, WEIGHED, "old_bank1"))
 TURNED = ((0, 256, "acc0"), (256, 512, "acc1"))
 FETCH = 256
 
@@ -77,10 +77,13 @@ def tile_picked_wema_tanh_l_kernel(tc, x_words, x_scales, mem, w1, old, new, slo
             return bank[:].rearrange("q c p -> q p c")
 
         old_rows = keep.tile([P, WEIGHED], F32, name="old_rows")
-        new_rows = keep.tile([P, WEIGHED], F32, name="new_rows")
         nc.scalar.copy(out=old_rows[:].rearrange("q (p c) -> q p c", c=4), in_=spread(old_cols[:, 0, :], "old_bank0"))
-        nc.scalar.copy(out=new_rows[:].rearrange("q (p c) -> q p c", c=4), in_=spread(new_cols[:], "new_bank"))
-        old_second = spread(old_cols[:, 1, :], "old_bank1")
+        old_later = keep.tile([P, T - WEIGHED], F32, name="old_later")
+        nc.scalar.copy(out=old_later[:].rearrange("q (p c) -> q p c", c=4), in_=spread(old_cols[:, 1, :], "old_bank1"))
+        new_bank = psum.tile([P, P, 4], F32, name="new_bank", tag="new_bank")
+        for c in range(4):
+            nc.tensor.transpose(new_bank[:, :, c], new_cols[:, c : c + 1].to_broadcast([P, P]), ident[:])
+        new_rows = new_bank[:].rearrange("q p c -> q (p c)")
 
         grouped = keep.tile([P, PASSES, M, 4], BF16, name="w_grouped", align_bytes=64)
         for z in range(PASSES):
@@ -107,12 +110,7 @@ def tile_picked_wema_tanh_l_kernel(tc, x_words, x_scales, mem, w1, old, new, slo
         for a in range(0, T - WEIGHED, FETCH):
             b = a + FETCH
             nc.scalar.activation(out=fetched[:, a:b], in_=entries(WEIGHED + a, WEIGHED + b), func=COPY)
-            nc.vector.tensor_tensor(
-                kept[:, WEIGHED + a : WEIGHED + b].rearrange("q (p c) -> q p c", c=4),
-                fetched[:, a:b].rearrange("q (p c) -> q p c", c=4),
-                old_second[:, a // 4 : b // 4, :],
-                MULT,
-            )
+            nc.vector.tensor_tensor(kept[:, WEIGHED + a : WEIGHED + b], fetched[:, a:b], old_later[:, a:b], MULT)
 
         y = old_rows
         for i, (a, b, tag) in enumerate(PIECES):

@@ -26,6 +26,7 @@ LOADS = ((0, 128), (128, WEIGHED), (WEIGHED, T))
 PIECES = ((0, 128, "acc0"), (128, 256, "acc1"), (256, 384, "old_bank0"), (384, WEIGHED, "old_bank1"))
 TURNED = ((0, 256, "acc0"), (256, 512, "acc1"))
 FETCH = 256
+BLOCKS = (T - WEIGHED) // P
 
 
 def tile_picked_wema_tanh_l_kernel(tc, x_words, x_scales, mem, w1, old, new, slot, out):
@@ -36,19 +37,23 @@ def tile_picked_wema_tanh_l_kernel(tc, x_words, x_scales, mem, w1, old, new, slo
 
         offsets = keep.tile([P, T // 16], U16, name="offsets")
         window = keep.tile([P, U], F32, name="window")
-        old_cols = keep.tile([P, 2, 4], F32, name="old_cols", tag="old_cols")
+        old_cols = keep.tile([P, 8], F32, name="old_cols", tag="old_cols")
         new_cols = keep.tile([P, 4], F32, name="new_cols")
-        new_scale = keep.tile([P, (T - WEIGHED) // P], F32, name="new_scale")
+        new_blocks = keep.tile([P, P], F32, name="new_blocks")
         ident = keep.tile([P, P], F32, name="ident")
         x_plane = keep.tile([P, PASSES, T], U8, name="x_plane", align_bytes=64)
-        w_raw = keep.tile([P, PASSES, 4, M], F32, name="w_raw")
+        w_raw = [keep.tile([P, 4, M], F32, name="w_raw%d" % z) for z in range(PASSES)]
 
         make_identity(nc, ident[:])
+        nc.vector.memset(new_blocks[:], 0.0)
 
-        nc.sync.dma_start(out=w_raw[:], in_=w1.rearrange("(z p j) m -> p z j m", z=PASSES, j=4))
-        nc.sync.dma_start(out=old_cols[:], in_=old[0].rearrange("(h p c) -> p h c", h=2, c=4))
+        w_rows = w1.rearrange("(z p j) m -> z p j m", z=PASSES, j=4)
+        nc.sync.dma_start(out=w_raw[0][:], in_=w_rows[0])
+        nc.sync.dma_start(out=old_cols[:], in_=old[0].rearrange("(p c) -> p c", c=8))
+        nc.sync.dma_start(out=w_raw[1][:], in_=w_rows[1])
         nc.sync.dma_start(out=new_cols[:], in_=new[0, 0:WEIGHED].rearrange("(p c) -> p c", c=4))
         nc.sync.dma_start(offsets[:], slot)
+        nc.sync.dma_start(out=new_blocks[0:BLOCKS, :], in_=new[1, WEIGHED:T].rearrange("(b p) -> b p", p=P))
         nc.sync.dma_start(out=window[:], in_=mem)
         scale_rows = x_scales.bitcast(I32)
         for q in range(4):
@@ -62,8 +67,6 @@ def tile_picked_wema_tanh_l_kernel(tc, x_words, x_scales, mem, w1, old, new, slo
             piece = keep.tile([P, PASSES, 2 * (b - a)], U8, name="x_codes%d" % i, align_bytes=64)
             nc.sync.dma_start(out=piece[:].bitcast(I32), in_=words[:, :, a // 2 : b // 2])
             x_codes.append(piece)
-        with nc.allow_non_contiguous_dma(reason="one weight for each partition and block"):
-            nc.sync.dma_start(out=new_scale[:], in_=new[1, WEIGHED:T].rearrange("(b p) -> p b", p=P))
 
         def codes_of(z, g):
             i = [a <= g < b for a, b in LOADS].index(True)
@@ -76,10 +79,16 @@ def tile_picked_wema_tanh_l_kernel(tc, x_words, x_scales, mem, w1, old, new, slo
                 nc.tensor.transpose(bank[:, c, :], cols[:, c : c + 1].to_broadcast([P, P]), ident[:])
             return bank[:].rearrange("q c p -> q p c")
 
-        old_rows = keep.tile([P, WEIGHED], F32, name="old_rows")
-        nc.scalar.copy(out=old_rows[:].rearrange("q (p c) -> q p c", c=4), in_=spread(old_cols[:, 0, :], "old_bank0"))
-        old_later = keep.tile([P, T - WEIGHED], F32, name="old_later")
-        nc.scalar.copy(out=old_later[:].rearrange("q (p c) -> q p c", c=4), in_=spread(old_cols[:, 1, :], "old_bank1"))
+        old_rows = keep.tile([P, T], F32, name="old_rows")
+        for h in range(2):
+            nc.scalar.copy(
+                out=old_rows[:].rearrange("q (p c) -> q p c", c=8)[:, :, 4 * h : 4 * h + 4],
+                in_=spread(old_cols[:, 4 * h : 4 * h + 4], "old_bank%d" % h),
+            )
+        new_turned = psum.tile([P, P], F32, name="new_turned", tag="new_turned")
+        nc.tensor.transpose(new_turned[:], new_blocks[:], ident[:])
+        new_scale = keep.tile([P, BLOCKS], F32, name="new_scale")
+        nc.scalar.copy(out=new_scale[:], in_=new_turned[:, 0:BLOCKS])
         new_bank = psum.tile([P, P, 4], F32, name="new_bank", tag="new_bank")
         for c in range(4):
             nc.tensor.transpose(new_bank[:, :, c], new_cols[:, c : c + 1].to_broadcast([P, P]), ident[:])
@@ -89,7 +98,7 @@ def tile_picked_wema_tanh_l_kernel(tc, x_words, x_scales, mem, w1, old, new, slo
         for z in range(PASSES):
             nc.vector.tensor_copy(
                 out=grouped[:, z].rearrange("p (c i) j -> p c j i", i=4),
-                in_=w_raw[:, z].rearrange("p j (c i) -> p c j i", i=4),
+                in_=w_raw[z][:].rearrange("p j (c i) -> p c j i", i=4),
             )
         w_words = keep.tile([P, PASSES, M], U32, name="w_words", align_bytes=64)
         w_plane = keep.tile([P, PASSES, M], U8, name="w_plane", align_bytes=64)
@@ -110,7 +119,7 @@ def tile_picked_wema_tanh_l_kernel(tc, x_words, x_scales, mem, w1, old, new, slo
         for a in range(0, T - WEIGHED, FETCH):
             b = a + FETCH
             nc.scalar.activation(out=fetched[:, a:b], in_=entries(WEIGHED + a, WEIGHED + b), func=COPY)
-            nc.vector.tensor_tensor(kept[:, WEIGHED + a : WEIGHED + b], fetched[:, a:b], old_later[:, a:b], MULT)
+            nc.vector.tensor_tensor(kept[:, WEIGHED + a : WEIGHED + b], fetched[:, a:b], old_rows[:, WEIGHED + a : WEIGHED + b], MULT)
 
         y = old_rows
         for i, (a, b, tag) in enumerate(PIECES):

@@ -23,10 +23,10 @@ FLOPS = 2 * K * T * M
 BYTES = 2 * 128 * 2048 + 2 * 16 * 1024 + 2 * M * U * 4 + K * M * 4 + 2 * T * 4 + 128 * 64 * 2
 WEIGHED = 512
 LOADS = ((0, 128), (128, WEIGHED), (WEIGHED, T))
-PIECES = ((0, 128, "acc0"), (128, 256, "acc1"), (256, 384, "old_bank0"), (384, WEIGHED, "old_bank1"))
-TURNED = ((0, 256, "acc0"), (256, 512, "acc1"))
+PIECES = ((0, 128, "turn_bank"), (128, 256, "old_bank0"), (256, 384, "old_bank1"), (384, WEIGHED, "turn_bank"))
+TURNED = ((0, 256, "old_bank0"), (256, 512, "old_bank1"))
 FETCH = 256
-BLOCKS = (T - WEIGHED) // P
+BLOCKS = T // P
 
 
 def tile_picked_wema_tanh_l_kernel(tc, x_words, x_scales, mem, w1, old, new, slot, out):
@@ -37,23 +37,20 @@ def tile_picked_wema_tanh_l_kernel(tc, x_words, x_scales, mem, w1, old, new, slo
 
         offsets = keep.tile([P, T // 16], U16, name="offsets")
         window = keep.tile([P, U], F32, name="window")
-        old_cols = keep.tile([P, 8], F32, name="old_cols", tag="old_cols")
-        new_cols = keep.tile([P, 4], F32, name="new_cols")
-        new_blocks = keep.tile([P, P], F32, name="new_blocks")
+        blocks = keep.tile([P, P], F32, name="blocks")
         ident = keep.tile([P, P], F32, name="ident")
         x_plane = keep.tile([P, PASSES, T], U8, name="x_plane", align_bytes=64)
         w_raw = [keep.tile([P, 4, M], F32, name="w_raw%d" % z) for z in range(PASSES)]
 
+        nc.gpsimd.memset(blocks[:], 0.0)
         make_identity(nc, ident[:])
-        nc.vector.memset(new_blocks[:], 0.0)
 
         w_rows = w1.rearrange("(z p j) m -> z p j m", z=PASSES, j=4)
         nc.sync.dma_start(out=w_raw[0][:], in_=w_rows[0])
-        nc.sync.dma_start(out=old_cols[:], in_=old[0].rearrange("(p c) -> p c", c=8))
-        nc.sync.dma_start(out=w_raw[1][:], in_=w_rows[1])
-        nc.sync.dma_start(out=new_cols[:], in_=new[0, 0:WEIGHED].rearrange("(p c) -> p c", c=4))
         nc.sync.dma_start(offsets[:], slot)
-        nc.sync.dma_start(out=new_blocks[0:BLOCKS, :], in_=new[1, WEIGHED:T].rearrange("(b p) -> b p", p=P))
+        nc.sync.dma_start(out=blocks[0:BLOCKS, :], in_=old[0].rearrange("(b p) -> b p", p=P))
+        nc.sync.dma_start(out=blocks[BLOCKS : 2 * BLOCKS, :], in_=new[0].rearrange("(b p) -> b p", p=P))
+        nc.sync.dma_start(out=w_raw[1][:], in_=w_rows[1])
         nc.sync.dma_start(out=window[:], in_=mem)
         scale_rows = x_scales.bitcast(I32)
         for q in range(4):
@@ -74,25 +71,23 @@ def tile_picked_wema_tanh_l_kernel(tc, x_words, x_scales, mem, w1, old, new, slo
             return x_codes[i][:, z, 2 * (g - first) : 2 * (g - first + P)].bitcast(FP4X4)
 
         def spread(cols, name):
-            bank = psum.tile([P, 4, P], F32, name=name, tag=name)
-            for c in range(4):
+            bank = psum.tile([P, cols.shape[1], P], F32, name=name, tag=name)
+            for c in range(cols.shape[1]):
                 nc.tensor.transpose(bank[:, c, :], cols[:, c : c + 1].to_broadcast([P, P]), ident[:])
-            return bank[:].rearrange("q c p -> q p c")
+            return bank[:].rearrange("q c p -> q (c p)")
 
-        old_rows = keep.tile([P, T], F32, name="old_rows")
+        turned = psum.tile([P, P], F32, name="turned", tag="turn_bank")
+        nc.tensor.transpose(turned[:], blocks[:], ident[:])
+        old_cols = keep.tile([P, BLOCKS], F32, name="old_cols", tag="old_cols")
+        new_cols = keep.tile([P, BLOCKS], F32, name="new_cols")
+        nc.scalar.copy(out=old_cols[:], in_=turned[:, 0:BLOCKS])
+        nc.scalar.copy(out=new_cols[:], in_=turned[:, BLOCKS : 2 * BLOCKS])
+        new_scale = new_cols[:, WEIGHED // P :]
+        old_rows = keep.tile([P, WEIGHED], F32, name="old_rows")
         for h in range(2):
-            nc.scalar.copy(
-                out=old_rows[:].rearrange("q (p c) -> q p c", c=8)[:, :, 4 * h : 4 * h + 4],
-                in_=spread(old_cols[:, 4 * h : 4 * h + 4], "old_bank%d" % h),
-            )
-        new_turned = psum.tile([P, P], F32, name="new_turned", tag="new_turned")
-        nc.tensor.transpose(new_turned[:], new_blocks[:], ident[:])
-        new_scale = keep.tile([P, BLOCKS], F32, name="new_scale")
-        nc.scalar.copy(out=new_scale[:], in_=new_turned[:, 0:BLOCKS])
-        new_bank = psum.tile([P, P, 4], F32, name="new_bank", tag="new_bank")
-        for c in range(4):
-            nc.tensor.transpose(new_bank[:, :, c], new_cols[:, c : c + 1].to_broadcast([P, P]), ident[:])
-        new_rows = new_bank[:].rearrange("q p c -> q (p c)")
+            nc.scalar.copy(out=old_rows[:, FETCH * h : FETCH * (h + 1)], in_=spread(old_cols[:, 2 * h : 2 * h + 2], "old_bank%d" % h))
+        old_later = spread(old_cols[:, 4:8], "old_later")
+        new_rows = spread(new_cols[:, 0:4], "new_bank")
 
         grouped = keep.tile([P, PASSES, M, 4], BF16, name="w_grouped", align_bytes=64)
         for z in range(PASSES):
@@ -119,7 +114,7 @@ def tile_picked_wema_tanh_l_kernel(tc, x_words, x_scales, mem, w1, old, new, slo
         for a in range(0, T - WEIGHED, FETCH):
             b = a + FETCH
             nc.scalar.activation(out=fetched[:, a:b], in_=entries(WEIGHED + a, WEIGHED + b), func=COPY)
-            nc.vector.tensor_tensor(kept[:, WEIGHED + a : WEIGHED + b], fetched[:, a:b], old_rows[:, WEIGHED + a : WEIGHED + b], MULT)
+            nc.vector.tensor_tensor(kept[:, WEIGHED + a : WEIGHED + b], fetched[:, a:b], old_later[:, a:b], MULT)
 
         y = old_rows
         for i, (a, b, tag) in enumerate(PIECES):

@@ -22,7 +22,8 @@ PASSES = 2
 FLOPS = 2 * K * T * M
 BYTES = 2 * 128 * 2048 + 2 * 16 * 1024 + 2 * M * U * 4 + K * M * 4 + 2 * T * 4 + 128 * 64 * 2
 WEIGHED = 512
-LOADS = ((0, 128), (128, WEIGHED), (WEIGHED, T))
+EARLY = 256
+LOADS = ((0, EARLY), (EARLY, T))
 PIECES = ((0, 128, "turn_bank"), (128, 256, "old_bank0"), (256, 384, "old_bank1"), (384, WEIGHED, "turn_bank"))
 TURNED = ((0, 256, "old_bank0"), (256, 512, "old_bank1"))
 FETCH = 256
@@ -39,36 +40,49 @@ def tile_picked_wema_tanh_l_kernel(tc, x_words, x_scales, mem, w1, old, new, slo
         window = keep.tile([P, U], F32, name="window")
         blocks = keep.tile([P, P], F32, name="blocks")
         ident = keep.tile([P, P], F32, name="ident")
-        x_plane = keep.tile([P, PASSES, T], U8, name="x_plane", align_bytes=64)
-        w_raw = [keep.tile([P, 4, M], F32, name="w_raw%d" % z) for z in range(PASSES)]
+        planes = [keep.tile([P, PASSES, b - a], U8, name="x_plane%d" % a, align_bytes=64) for a, b in LOADS]
+        w_raw = keep.tile([P, PASSES, 4, M], F32, name="w_raw")
 
         nc.gpsimd.memset(blocks[:], 0.0)
         make_identity(nc, ident[:])
 
-        w_rows = w1.rearrange("(z p j) m -> z p j m", z=PASSES, j=4)
-        nc.sync.dma_start(out=w_raw[0][:], in_=w_rows[0])
-        nc.sync.dma_start(offsets[:], slot)
-        nc.sync.dma_start(out=blocks[0:BLOCKS, :], in_=old[0].rearrange("(b p) -> b p", p=P))
-        nc.sync.dma_start(out=blocks[BLOCKS : 2 * BLOCKS, :], in_=new[0].rearrange("(b p) -> b p", p=P))
-        nc.sync.dma_start(out=w_raw[1][:], in_=w_rows[1])
-        nc.sync.dma_start(out=window[:], in_=mem)
         scale_rows = x_scales.bitcast(I32)
-        for q in range(4):
-            nc.sync.dma_start(
-                out=x_plane[32 * q : 32 * q + 4, :, :].bitcast(I32),
-                in_=scale_rows[:, 4 * q : 4 * q + 4, :].rearrange("z r c -> r z c"),
-            )
         words = x_words.bitcast(I32).rearrange("z p c -> p z c")
-        x_codes = []
-        for i, (a, b) in enumerate(LOADS):
-            piece = keep.tile([P, PASSES, 2 * (b - a)], U8, name="x_codes%d" % i, align_bytes=64)
-            nc.sync.dma_start(out=piece[:].bitcast(I32), in_=words[:, :, a // 2 : b // 2])
-            x_codes.append(piece)
+        x_codes = [keep.tile([P, PASSES, 2 * (b - a)], U8, name="x_codes%d" % a, align_bytes=64) for a, b in LOADS]
+
+        def load_scales(i, q):
+            a, b = LOADS[i]
+            nc.sync.dma_start(
+                out=planes[i][32 * q : 32 * q + 4, :, :].bitcast(I32),
+                in_=scale_rows[:, 4 * q : 4 * q + 4, a // 4 : b // 4].rearrange("z r c -> r z c"),
+            )
+
+        def load_codes(i):
+            a, b = LOADS[i]
+            nc.sync.dma_start(out=x_codes[i][:].bitcast(I32), in_=words[:, :, a // 2 : b // 2])
+
+        nc.sync.dma_start(out=w_raw[:], in_=w1.rearrange("(z p j) m -> p z j m", z=PASSES, j=4))
+        nc.scalar.dma_start(out=blocks[0:BLOCKS, :], in_=old[0].rearrange("(b p) -> b p", p=P))
+        nc.scalar.dma_start(out=blocks[BLOCKS : 2 * BLOCKS, :], in_=new[0].rearrange("(b p) -> b p", p=P))
+        nc.sync.dma_start(offsets[:], slot)
+        for q in (0, 2, 1):
+            load_scales(0, q)
+        nc.sync.dma_start(out=window[:], in_=mem)
+        load_scales(0, 3)
+        load_codes(0)
+        for q in (0, 2, 1, 3):
+            load_scales(1, q)
+        load_codes(1)
 
         def codes_of(z, g):
             i = [a <= g < b for a, b in LOADS].index(True)
             first = LOADS[i][0]
             return x_codes[i][:, z, 2 * (g - first) : 2 * (g - first + P)].bitcast(FP4X4)
+
+        def scales_of(z, g):
+            i = [a <= g < b for a, b in LOADS].index(True)
+            first = LOADS[i][0]
+            return planes[i][:, z, g - first : g - first + P]
 
         def spread(cols, name):
             bank = psum.tile([P, cols.shape[1], P], F32, name=name, tag=name)
@@ -93,7 +107,7 @@ def tile_picked_wema_tanh_l_kernel(tc, x_words, x_scales, mem, w1, old, new, slo
         for z in range(PASSES):
             nc.vector.tensor_copy(
                 out=grouped[:, z].rearrange("p (c i) j -> p c j i", i=4),
-                in_=w_raw[z][:].rearrange("p j (c i) -> p c j i", i=4),
+                in_=w_raw[:, z].rearrange("p j (c i) -> p c j i", i=4),
             )
         w_words = keep.tile([P, PASSES, M], U32, name="w_words", align_bytes=64)
         w_plane = keep.tile([P, PASSES, M], U8, name="w_plane", align_bytes=64)
@@ -126,7 +140,7 @@ def tile_picked_wema_tanh_l_kernel(tc, x_words, x_scales, mem, w1, old, new, slo
                         lhsT=w_words[:, z, :].bitcast(FP8X4),
                         lhsT_scale=w_plane[:, z, :],
                         rhs=codes_of(z, g),
-                        rhs_scale=x_plane[:, z, g : g + P],
+                        rhs_scale=scales_of(z, g),
                         start=(z == 0),
                         stop=(z == PASSES - 1),
                     )
@@ -142,7 +156,7 @@ def tile_picked_wema_tanh_l_kernel(tc, x_words, x_scales, mem, w1, old, new, slo
                     nc.tensor.matmul_mx(
                         out=acc_t[:, g - a : g - a + P],
                         lhsT=codes_of(z, WEIGHED + g),
-                        lhsT_scale=x_plane[:, z, WEIGHED + g : WEIGHED + g + P],
+                        lhsT_scale=scales_of(z, WEIGHED + g),
                         rhs=w_words[:, z, :].bitcast(FP8X4),
                         rhs_scale=w_plane[:, z, :],
                         start=(z == 0),
@@ -165,8 +179,8 @@ def tile_picked_wema_tanh_l_kernel(tc, x_words, x_scales, mem, w1, old, new, slo
 
         weigh(0, 128)
         weigh(128, 256)
-        weigh(256, 384)
         scatter(0, 128)
+        weigh(256, 384)
         weigh(384, WEIGHED)
         scatter(128, 384)
         scatter(384, T)

@@ -65,14 +65,14 @@ def tile_picked_wema_tanh_l_kernel(tc, x_words, x_scales, mem, w1, old, new, slo
         nc.scalar.dma_start(out=blocks[0:BLOCKS, :], in_=old[0].rearrange("(b p) -> b p", p=P))
         nc.scalar.dma_start(out=blocks[BLOCKS : 2 * BLOCKS, :], in_=new[0].rearrange("(b p) -> b p", p=P))
         nc.sync.dma_start(offsets[:], slot)
-        for q in (0, 2, 1):
-            load_scales(0, q)
+        load_scales(0, 0)
         nc.sync.dma_start(out=window[:], in_=mem)
-        load_scales(0, 3)
+        for q in (2, 1, 3):
+            load_scales(0, q)
         load_codes(0)
+        load_codes(1)
         for q in (0, 2, 1, 3):
             load_scales(1, q)
-        load_codes(1)
 
         def codes_of(z, g):
             i = [a <= g < b for a, b in LOADS].index(True)

@@ -62,8 +62,8 @@ def tile_picked_wema_tanh_l_kernel(tc, x_words, x_scales, mem, w1, old, new, slo
             nc.sync.dma_start(out=x_codes[i][:].bitcast(I32), in_=words[:, :, a // 2 : b // 2])
 
         nc.sync.dma_start(out=w_raw[:], in_=w1.rearrange("(z p j) m -> p z j m", z=PASSES, j=4))
-        nc.scalar.dma_start(out=blocks[0:BLOCKS, :], in_=old[0].rearrange("(b p) -> b p", p=P))
-        nc.scalar.dma_start(out=blocks[BLOCKS : 2 * BLOCKS, :], in_=new[0].rearrange("(b p) -> b p", p=P))
+        nc.sync.dma_start(out=blocks[0:BLOCKS, :], in_=old[0].rearrange("(b p) -> b p", p=P))
+        nc.sync.dma_start(out=blocks[BLOCKS : 2 * BLOCKS, :], in_=new[0].rearrange("(b p) -> b p", p=P))
         nc.sync.dma_start(offsets[:], slot)
         load_scales(0, 0)
         nc.sync.dma_start(out=window[:], in_=mem)

@@ -24,10 +24,12 @@ BYTES = 2 * 128 * 2048 + 2 * 16 * 1024 + 2 * M * U * 4 + K * M * 4 + 2 * T * 4 +
 WEIGHED = 512
 EARLY = 256
 LOADS = ((0, EARLY), (EARLY, T))
+SCALE_LOADS = ((0, WEIGHED), (WEIGHED, T))
 PIECES = ((0, 128, "turn_bank"), (128, 256, "old_bank0"), (256, 384, "old_bank1"), (384, WEIGHED, "turn_bank"))
 TURNED = ((0, 256, "old_bank0"), (256, 512, "old_bank1"))
 FETCH = 256
 BLOCKS = T // P
+HELD = 7
 
 
 def tile_picked_wema_tanh_l_kernel(tc, x_words, x_scales, mem, w1, old, new, slot, out):
@@ -40,7 +42,7 @@ def tile_picked_wema_tanh_l_kernel(tc, x_words, x_scales, mem, w1, old, new, slo
         window = keep.tile([P, U], F32, name="window")
         blocks = keep.tile([P, P], F32, name="blocks")
         ident = keep.tile([P, P], F32, name="ident")
-        planes = [keep.tile([P, PASSES, b - a], U8, name="x_plane%d" % a, align_bytes=64) for a, b in LOADS]
+        planes = [keep.tile([P, PASSES, b - a], U8, name="x_plane%d" % a, align_bytes=64) for a, b in SCALE_LOADS]
         w_raw = keep.tile([P, PASSES, 4, M], F32, name="w_raw")
 
         nc.gpsimd.memset(blocks[:], 0.0)
@@ -51,7 +53,7 @@ def tile_picked_wema_tanh_l_kernel(tc, x_words, x_scales, mem, w1, old, new, slo
         x_codes = [keep.tile([P, PASSES, 2 * (b - a)], U8, name="x_codes%d" % a, align_bytes=64) for a, b in LOADS]
 
         def load_scales(i, q):
-            a, b = LOADS[i]
+            a, b = SCALE_LOADS[i]
             nc.sync.dma_start(
                 out=planes[i][32 * q : 32 * q + 4, :, :].bitcast(I32),
                 in_=scale_rows[:, 4 * q : 4 * q + 4, a // 4 : b // 4].rearrange("z r c -> r z c"),
@@ -80,28 +82,29 @@ def tile_picked_wema_tanh_l_kernel(tc, x_words, x_scales, mem, w1, old, new, slo
             return x_codes[i][:, z, 2 * (g - first) : 2 * (g - first + P)].bitcast(FP4X4)
 
         def scales_of(z, g):
-            i = [a <= g < b for a, b in LOADS].index(True)
-            first = LOADS[i][0]
+            i = [a <= g < b for a, b in SCALE_LOADS].index(True)
+            first = SCALE_LOADS[i][0]
             return planes[i][:, z, g - first : g - first + P]
 
         def spread(cols, name):
-            bank = psum.tile([P, cols.shape[1], P], F32, name=name, tag=name)
-            for c in range(cols.shape[1]):
-                nc.tensor.transpose(bank[:, c, :], cols[:, c : c + 1].to_broadcast([P, P]), ident[:])
+            bank = psum.tile([P, len(cols), P], F32, name=name, tag=name)
+            for c, col in enumerate(cols):
+                nc.tensor.transpose(bank[:, c, :], col.to_broadcast([P, P]), ident[:])
             return bank[:].rearrange("q c p -> q (c p)")
 
         turned = psum.tile([P, P], F32, name="turned", tag="turn_bank")
         nc.tensor.transpose(turned[:], blocks[:], ident[:])
-        old_cols = keep.tile([P, BLOCKS], F32, name="old_cols", tag="old_cols")
-        new_cols = keep.tile([P, BLOCKS], F32, name="new_cols")
-        nc.scalar.copy(out=old_cols[:], in_=turned[:, 0:BLOCKS])
-        nc.scalar.copy(out=new_cols[:], in_=turned[:, BLOCKS : 2 * BLOCKS])
-        new_scale = new_cols[:, WEIGHED // P :]
+        first_cols = keep.tile([P, HELD], F32, name="first_cols", tag="old_cols")
+        other_cols = keep.tile([P, 2 * BLOCKS - HELD], F32, name="other_cols")
+        nc.scalar.copy(out=first_cols[:], in_=turned[:, 0:HELD])
+        nc.scalar.copy(out=other_cols[:], in_=turned[:, HELD : 2 * BLOCKS])
+        columns = [first_cols[:, c : c + 1] for c in range(HELD)] + [other_cols[:, c : c + 1] for c in range(2 * BLOCKS - HELD)]
+        new_scale = other_cols[:, BLOCKS - HELD + WEIGHED // P :]
         old_rows = keep.tile([P, WEIGHED], F32, name="old_rows")
-        for h in range(2):
-            nc.scalar.copy(out=old_rows[:, FETCH * h : FETCH * (h + 1)], in_=spread(old_cols[:, 2 * h : 2 * h + 2], "old_bank%d" % h))
-        old_later = spread(old_cols[:, 4:8], "old_later")
-        new_rows = spread(new_cols[:, 0:4], "new_bank")
+        for h, copy_rows in enumerate((nc.vector.tensor_copy, nc.scalar.copy)):
+            copy_rows(out=old_rows[:, FETCH * h : FETCH * (h + 1)], in_=spread(columns[2 * h : 2 * h + 2], "old_bank%d" % h))
+        old_later = spread(columns[4:8], "old_later")
+        new_rows = spread(columns[BLOCKS : BLOCKS + 4], "new_bank")
 
         grouped = keep.tile([P, PASSES, M, 4], BF16, name="w_grouped", align_bytes=64)
         for z in range(PASSES):

@@ -131,7 +131,13 @@ def tile_picked_wema_tanh_l_kernel(tc, x_words, x_scales, mem, w1, old, new, slo
         for a in range(0, T - WEIGHED, FETCH):
             b = a + FETCH
             nc.scalar.activation(out=fetched[:, a:b], in_=entries(WEIGHED + a, WEIGHED + b), func=COPY)
+
+        def keep_old(a, b):
             nc.vector.tensor_tensor(kept[:, WEIGHED + a : WEIGHED + b], fetched[:, a:b], old_later[:, a:b], MULT)
+
+        keep_old(0, FETCH)
+        no_bias = kept[:, T - 1 : T]
+        nc.gpsimd.memset(no_bias, 0.0)
 
         y = old_rows
         for i, (a, b, tag) in enumerate(PIECES):
@@ -147,7 +153,7 @@ def tile_picked_wema_tanh_l_kernel(tc, x_words, x_scales, mem, w1, old, new, slo
                         start=(z == 0),
                         stop=(z == PASSES - 1),
                     )
-            nc.scalar.activation(out=y[:, a:b], in_=acc[:], func=TANH)
+            nc.scalar.activation(out=y[:, a:b], in_=acc[:], func=TANH, bias=no_bias if i == 0 else 0.0)
 
         moved = keep.tile([P, T], F32, name="moved")
         y_t = keep.tile([P, T - WEIGHED], F32, name="y_t")
@@ -181,8 +187,9 @@ def tile_picked_wema_tanh_l_kernel(tc, x_words, x_scales, mem, w1, old, new, slo
             nc.vector.tensor_tensor(entries(a, b), kept[:, a:b], moved[:, a:b], ADD)
 
         weigh(0, 128)
-        weigh(128, 256)
+        keep_old(FETCH, 2 * FETCH)
         scatter(0, 128)
+        weigh(128, 256)
         weigh(256, 384)
         weigh(384, WEIGHED)
         scatter(128, 384)

from contextlib import ExitStack

import concourse.mybir as mybir
from concourse.masks import make_identity

F32 = mybir.dt.float32
BF16 = mybir.dt.bfloat16
I32 = mybir.dt.int32
U32 = mybir.dt.uint32
U16 = mybir.dt.uint16
U8 = mybir.dt.uint8
FP8X4 = mybir.dt.float8_e4m3fn_x4
FP4X4 = mybir.dt.float4_e2m1fn_x4
MULT = mybir.AluOpType.mult
ADD = mybir.AluOpType.add
TANH = mybir.ActivationFunctionType.Tanh
COPY = mybir.ActivationFunctionType.Copy

P = 128
K, T, M, U = 1024, 1024, 128, 2048
PASSES = 2
FLOPS = 2 * K * T * M
BYTES = 2 * 128 * 2048 + 2 * 16 * 1024 + 2 * M * U * 4 + K * M * 4 + 2 * T * 4 + 128 * 64 * 2
WEIGHED = 512
EARLY = 256
LOADS = ((0, EARLY), (EARLY, T))
SCALE_LOADS = ((0, WEIGHED), (WEIGHED, T))
PIECES = ((0, 128, "turn_bank"), (128, 256, "old_bank0"), (256, 384, "old_bank1"), (384, WEIGHED, "turn_bank"))
TURNED = ((0, 256, "old_bank0"), (256, 512, "old_bank1"))
FETCH = 256
BLOCKS = T // P
HELD = 7


def tile_picked_wema_tanh_l_kernel(tc, x_words, x_scales, mem, w1, old, new, slot, out):
    nc = tc.nc
    with ExitStack() as ctx:
        keep = ctx.enter_context(tc.tile_pool(name="keep", bufs=1))
        psum = ctx.enter_context(tc.psum_pool(name="psum", bufs=1))

        offsets = keep.tile([P, T // 16], U16, name="offsets")
        window = keep.tile([P, U], F32, name="window")
        blocks = keep.tile([P, P], F32, name="blocks")
        ident = keep.tile([P, P], F32, name="ident")
        planes = [keep.tile([P, PASSES, b - a], U8, name="x_plane%d" % a, align_bytes=64) for a, b in SCALE_LOADS]
        w_raw = keep.tile([P, PASSES, 4, M], F32, name="w_raw")

        nc.gpsimd.memset(blocks[:], 0.0)
        make_identity(nc, ident[:])

        scale_rows = x_scales.bitcast(I32)
        words = x_words.bitcast(I32).rearrange("z p c -> p z c")
        x_codes = [keep.tile([P, PASSES, 2 * (b - a)], U8, name="x_codes%d" % a, align_bytes=64) for a, b in LOADS]

        def load_scales(i, q):
            a, b = SCALE_LOADS[i]
            nc.sync.dma_start(
                out=planes[i][32 * q : 32 * q + 4, :, :].bitcast(I32),
                in_=scale_rows[:, 4 * q : 4 * q + 4, a // 4 : b // 4].rearrange("z r c -> r z c"),
            )

        def load_codes(i):
            a, b = LOADS[i]
            nc.sync.dma_start(out=x_codes[i][:].bitcast(I32), in_=words[:, :, a // 2 : b // 2])

        nc.sync.dma_start(out=w_raw[:], in_=w1.rearrange("(z p j) m -> p z j m", z=PASSES, j=4))
        nc.sync.dma_start(out=blocks[0:BLOCKS, :], in_=old[0].rearrange("(b p) -> b p", p=P))
        nc.sync.dma_start(out=blocks[BLOCKS : 2 * BLOCKS, :], in_=new[0].rearrange("(b p) -> b p", p=P))
        nc.sync.dma_start(offsets[:], slot)
        load_scales(0, 0)
        nc.sync.dma_start(out=window[:], in_=mem)
        for q in (2, 1, 3):
            load_scales(0, q)
        load_codes(0)
        load_codes(1)
        for q in (0, 2, 1, 3):
            load_scales(1, q)

        def codes_of(z, g):
            i = [a <= g < b for a, b in LOADS].index(True)
            first = LOADS[i][0]
            return x_codes[i][:, z, 2 * (g - first) : 2 * (g - first + P)].bitcast(FP4X4)

        def scales_of(z, g):
            i = [a <= g < b for a, b in SCALE_LOADS].index(True)
            first = SCALE_LOADS[i][0]
            return planes[i][:, z, g - first : g - first + P]

        def spread(cols, name):
            bank = psum.tile([P, len(cols), P], F32, name=name, tag=name)
            for c, col in enumerate(cols):
                nc.tensor.transpose(bank[:, c, :], col.to_broadcast([P, P]), ident[:])
            return bank[:].rearrange("q c p -> q (c p)")

        turned = psum.tile([P, P], F32, name="turned", tag="turn_bank")
        nc.tensor.transpose(turned[:], blocks[:], ident[:])
        first_cols = keep.tile([P, HELD], F32, name="first_cols", tag="old_cols")
        other_cols = keep.tile([P, 2 * BLOCKS - HELD], F32, name="other_cols")
        nc.scalar.copy(out=first_cols[:], in_=turned[:, 0:HELD])
        nc.scalar.copy(out=other_cols[:], in_=turned[:, HELD : 2 * BLOCKS])
        columns = [first_cols[:, c : c + 1] for c in range(HELD)] + [other_cols[:, c : c + 1] for c in range(2 * BLOCKS - HELD)]
        new_scale = other_cols[:, BLOCKS - HELD + WEIGHED // P :]
        old_rows = keep.tile([P, WEIGHED], F32, name="old_rows")
        for h, copy_rows in enumerate((nc.vector.tensor_copy, nc.scalar.copy)):
            copy_rows(out=old_rows[:, FETCH * h : FETCH * (h + 1)], in_=spread(columns[2 * h : 2 * h + 2], "old_bank%d" % h))
        old_later = spread(columns[4:8], "old_later")
        new_rows = spread(columns[BLOCKS : BLOCKS + 4], "new_bank")

        grouped = keep.tile([P, PASSES, M, 4], BF16, name="w_grouped", align_bytes=64)
        for z in range(PASSES):
            nc.vector.tensor_copy(
                out=grouped[:, z].rearrange("p (c i) j -> p c j i", i=4),
                in_=w_raw[:, z].rearrange("p j (c i) -> p c j i", i=4),
            )
        w_words = keep.tile([P, PASSES, M], U32, name="w_words", align_bytes=64)
        w_plane = keep.tile([P, PASSES, M], U8, name="w_plane", align_bytes=64)
        nc.vector.quantize_mx(
            out=w_words[:].rearrange("p z m -> p (z m)").bitcast(FP8X4),
            scales=w_plane[:].rearrange("p z m -> p (z m)"),
            in_=grouped[:].rearrange("p z m j -> p (z m j)"),
        )

        kept = keep.tile([P, T], F32, name="kept")
        fetched = keep.tile([P, T - WEIGHED], F32, name="fetched", tag="old_cols")

        def entries(a, b):
            return window[:].indirect(offsets[:, a // 16 : b // 16])

        for a in range(0, WEIGHED, FETCH):
            nc.vector.tensor_tensor(kept[:, a : a + FETCH], entries(a, a + FETCH), old_rows[:, a : a + FETCH], MULT)
        for a in range(0, T - WEIGHED, FETCH):
            b = a + FETCH
            nc.scalar.activation(out=fetched[:, a:b], in_=entries(WEIGHED + a, WEIGHED + b), func=COPY)

        def keep_old(a, b):
            nc.vector.tensor_tensor(kept[:, WEIGHED + a : WEIGHED + b], fetched[:, a:b], old_later[:, a:b], MULT)

        keep_old(0, FETCH)
        no_bias = kept[:, T - 1 : T]
        nc.gpsimd.memset(no_bias, 0.0)

        y = old_rows
        for i, (a, b, tag) in enumerate(PIECES):
            acc = psum.tile([P, b - a], F32, name="acc%d" % i, tag=tag)
            for g in range(a, b, P):
                for z in range(PASSES):
                    nc.tensor.matmul_mx(
                        out=acc[:, g - a : g - a + P],
                        lhsT=w_words[:, z, :].bitcast(FP8X4),
                        lhsT_scale=w_plane[:, z, :],
                        rhs=codes_of(z, g),
                        rhs_scale=scales_of(z, g),
                        start=(z == 0),
                        stop=(z == PASSES - 1),
                    )
            nc.scalar.activation(out=y[:, a:b], in_=acc[:], func=TANH, bias=no_bias if i == 0 else 0.0)

        moved = keep.tile([P, T], F32, name="moved")
        y_t = keep.tile([P, T - WEIGHED], F32, name="y_t")
        moved_t = keep.tile([P, T - WEIGHED], F32, name="moved_t")
        for h, (a, b, tag) in enumerate(TURNED):
            acc_t = psum.tile([P, b - a], F32, name="acc_t%d" % h, tag=tag)
            for g in range(a, b, P):
                for z in range(PASSES):
                    nc.tensor.matmul_mx(
                        out=acc_t[:, g - a : g - a + P],
                        lhsT=codes_of(z, WEIGHED + g),
                        lhsT_scale=scales_of(z, WEIGHED + g),
                        rhs=w_words[:, z, :].bitcast(FP8X4),
                        rhs_scale=w_plane[:, z, :],
                        start=(z == 0),
                        stop=(z == PASSES - 1),
                    )
            nc.scalar.activation(out=y_t[:, a:b], in_=acc_t[:], func=TANH)
        for g in range(0, T - WEIGHED, P):
            nc.scalar.activation(out=moved_t[:, g : g + P], in_=y_t[:, g : g + P], func=COPY, scale=new_scale[:, g // P : g // P + 1])
        for h, (a, b, tag) in enumerate(TURNED):
            back = psum.tile([P, b - a], F32, name="back%d" % h, tag="back%d" % h)
            for g in range(a, b, P):
                nc.tensor.transpose(back[:, g - a : g - a + P], moved_t[:, g : g + P], ident[:])
            nc.scalar.copy(out=moved[:, WEIGHED + a : WEIGHED + b], in_=back[:])

        def weigh(a, b):
            nc.vector.tensor_tensor(moved[:, a:b], y[:, a:b], new_rows[:, a:b], MULT)

        def scatter(a, b):
            nc.vector.tensor_tensor(entries(a, b), kept[:, a:b], moved[:, a:b], ADD)

        weigh(0, 128)
        keep_old(FETCH, 2 * FETCH)
        scatter(0, 128)
        weigh(128, 256)
        weigh(256, 384)
        weigh(384, WEIGHED)
        scatter(128, 384)
        scatter(384, T)
        nc.sync.dma_start(out=out, in_=window[:])
